import numpy as np
import ml_dtypes


def mxq(x, axis, fmt="e4m3"):
    dtype, down = {"e4m3": (ml_dtypes.float8_e4m3fn, 7), "e5m2": (ml_dtypes.float8_e5m2, 14)}[fmt]
    v = np.moveaxis(np.asarray(x, np.float32).astype(ml_dtypes.bfloat16).astype(np.float64), axis, -1)
    blocks = v.reshape(v.shape[:-1] + (-1, 32))
    amax = np.abs(blocks).max(-1, keepdims=True)
    byte = np.maximum(np.where(amax > 0, np.frexp(amax)[1] - 1 + 127, 0) - down, 1)
    scale = np.exp2(byte - 127.0)
    codes = (blocks / scale).astype(np.float32).astype(dtype).astype(np.float64)
    return np.moveaxis((codes * scale).reshape(v.shape), -1, axis)


WIDE = False


def mx_kscale(k):
    if not WIDE:
        return np.ones(k)
    levels = np.array([10, -10, 5, -5, 0])
    if k % 512:
        return np.exp2(np.random.permutation(np.resize(levels, k // 32))).repeat(32)
    a = np.empty((k // 512, 16))
    for p in range(k // 512):
        a[p, :8] = np.random.permutation(np.resize(levels, 8))
        for g in range(8):
            far = levels[np.abs(levels - a[p, g]) >= 10]
            a[p, g + 8] = far[np.random.randint(len(far))]
    return np.exp2(a.ravel()).repeat(32)


def f64(x):
    return np.asarray(x).astype(np.float64)


def striped(idx):
    return np.tile(idx.reshape(-1, 16).T, (8, 1)).astype(np.uint16)


def unstriped(offs):
    return offs[:16].T.reshape(-1).astype(np.int64)


def striped8(idx):
    return np.concatenate([v.reshape(-1, 16).T for v in idx]).astype(np.uint16)


def unstriped8(offs):
    return np.stack([offs[16 * g:16 * g + 16].T.reshape(-1) for g in range(8)]).astype(np.int64)


E2M1 = np.array([0.0, 0.5, 1.0, 1.5, 2.0, 3.0, 4.0, 6.0, -0.0, -0.5, -1.0, -1.5, -2.0, -3.0, -4.0, -6.0])


def pack_weight(w, fmt):
    k, n = w.shape
    w = f64(np.asarray(w, np.float32).astype(ml_dtypes.bfloat16)).reshape(k // 32, 32, n)
    amax = np.abs(w).max(1)
    if fmt == "e4m3":
        byte = np.frexp(amax)[1] - 1 + 127 - 7
    else:
        mant, ex = np.frexp(amax / 6.0)
        byte = np.where(mant > 0.5, ex, ex - 1) + 127
    byte = np.clip(np.where(amax > 0, byte, 1), 1, 254)
    scaled = (w * np.exp2(127.0 - byte)[:, None, :]).reshape(k, n).astype(np.float32)
    by_word = np.ascontiguousarray(scaled.reshape(k // 512, 128, 4, n).transpose(0, 1, 3, 2))
    if fmt == "e4m3":
        words = by_word.astype(ml_dtypes.float8_e4m3fn).view(np.uint8)
    else:
        c = by_word.astype(ml_dtypes.float4_e2m1fn).view(np.uint8) & 0xF
        words = (c[..., 0::2] | (c[..., 1::2] << 4)).reshape(k // 512, 128, 2 * n)
    return np.ascontiguousarray(words), np.ascontiguousarray(byte.astype(np.uint8).reshape(k // 512, 16, n))


def unpack_weight(words, scales, fmt):
    g, _, n = scales.shape
    words = np.ascontiguousarray(words).reshape(g, 128, n, -1)
    if fmt == "e4m3":
        vals = words.view(ml_dtypes.float8_e4m3fn).astype(np.float64)
    else:
        nib = np.empty((g, 128, n, 4), np.uint8)
        nib[..., 0::2] = words & 0xF
        nib[..., 1::2] = words >> 4
        vals = E2M1[nib]
    vals = vals * np.repeat(np.exp2(scales.astype(np.float64) - 127.0), 8, axis=1)[..., None]
    return vals.transpose(0, 1, 3, 2).reshape(g * 512, n)


def pack_table(v):
    words, scales = pack_weight(v, "e4m3")
    return np.concatenate([words.reshape(words.shape[0], -1), scales.reshape(scales.shape[0], -1)], axis=1)


def unpack_table(tab):
    g, t = tab.shape[0], tab.shape[1] // 528
    return unpack_weight(tab[:, :512 * t].reshape(g, 128, t, 4), tab[:, 512 * t:].reshape(g, 16, t), "e4m3")


def silu(v):
    return v / (1.0 + np.exp(-np.maximum(v, -700.0)))


K, M, T, S = 1024, 1024, 2048, 1024


def setup_inputs():
    n = np.random.standard_normal
    s = mx_kscale(K)[:, None]
    u = mx_kscale(512)[:, None]
    p_w4 = pack_weight(n((K, M)) / np.sqrt(K) / s, "e2m1")
    return {
        "tab": pack_table(n((K, T)) * s),
        "w4_words": p_w4[0],
        "w4_scales": p_w4[1],
        "down": (n((K, 512)) / np.sqrt(K) / s * u.T).astype(np.float32),
        "up": (0.5 * n((512, M)) / np.sqrt(512) / u).astype(np.float32),
        "b": (0.3 * n(1024)).astype(np.float32),
        "wgo": np.repeat(np.random.uniform(0.5, 2.0, (8, S)), 16, axis=0).astype(np.float32),
        "offs": striped(np.random.permutation(T)[:S]),
        "offs2": striped8(np.stack([np.random.permutation(T)[:S] for _ in range(8)])),
    }


def reference(tab, w4_words, w4_scales, down, up, b, wgo, offs, offs2):
    tab_ = unpack_table(tab)[:, unstriped(offs)]
    w4_ = unpack_weight(w4_words, w4_scales, "e2m1")
    down_ = mxq(f64(down), 0, "e4m3")
    up_ = mxq(f64(up), 0, "e4m3")
    h_ = mxq(down_.T @ tab_, 0, "e4m3")
    y = w4_.T @ tab_ + up_.T @ h_
    place = unstriped8(offs2)[np.arange(M) % 128 // 16]
    out = np.zeros((M, T))
    out[np.arange(M)[:, None], place] = f64(wgo)[np.arange(M) % 128] * (silu(y + f64(b)[:, None]))
    return out

@@ -1,0 +1,256 @@
+from contextlib import ExitStack
+
+import concourse.mybir as mybir
+from concourse.masks import make_identity
+
+K, M, T, S, R = 1024, 1024, 2048, 1024, 512
+FLOPS = 2 * K * M * S + 2 * K * R * S + 2 * R * M * S
+
+F32 = mybir.dt.float32
+BF16 = mybir.dt.bfloat16
+I32 = mybir.dt.int32
+U32 = mybir.dt.uint32
+U16 = mybir.dt.uint16
+U8 = mybir.dt.uint8
+FP8X4 = mybir.dt.float8_e4m3fn_x4
+FP4X4 = mybir.dt.float4_e2m1fn_x4
+SILU = mybir.ActivationFunctionType.Silu
+MULT = mybir.AluOpType.mult
+
+P = 128
+PACK = 4
+PASSES = K // (P * PACK)
+TILES = M // P
+LIST = 16
+BANK = 512
+HEAD_CHUNKS = ((0, 128), (128, 128), (256, 256), (512, 512))
+LAST_GATHERS = ((0, 256), (256, 256), (512, 512))
+UP_GROUPS = ((0, 1), (1, 1), (2, 2), (4, 2), (6, 2))
+PAGES = 3
+
+
+def tile_list_tabhs_l_silu_kernel(
+    tc, tab, w4_words, w4_scales, down, up, b, wgo, offs, offs2, out
+):
+    nc = tc.nc
+    with ExitStack() as ctx:
+        keep = ctx.enter_context(tc.tile_pool(name="keep", bufs=1))
+        hps = ctx.enter_context(tc.psum_pool(name="hps", bufs=3))
+        yps = ctx.enter_context(tc.psum_pool(name="yps", bufs=4))
+        bps = ctx.enter_context(tc.psum_pool(name="bps", bufs=1))
+
+        def tile(name, shape, dtype, tag=""):
+            return keep.tile(shape, dtype, name=name, tag=tag or name, align_bytes=64)
+
+        pick = keep.tile([P, S // LIST], U16, name="pick")
+        place = keep.tile([P, S // LIST], U16, name="place")
+        nc.sync.dma_start(pick[:], offs)
+
+        tab_scales = tile("tab_scales", [P, T], U8, "window")
+        for a in range(PASSES):
+            nc.sync.dma_start(
+                tab_scales[16 * a:16 * (a + 1), :].bitcast(I32),
+                tab[a, P * PACK * T:].rearrange("(q c) -> q c", q=16).bitcast(I32))
+        nc.sync.dma_start(place[:], offs2)
+        nc.gpsimd.memset(tab_scales[32:64, :].bitcast(I32), 0)
+        nc.gpsimd.memset(tab_scales[64:128, :].bitcast(I32), 0)
+
+        down_raw = [tile("down_raw%d" % a, [P, PACK, R], F32) for a in range(PASSES)]
+        tab_words = {}
+
+        def load_down(a):
+            nc.sync.dma_start(down_raw[a][:], down[512 * a:512 * (a + 1), :].rearrange("(p j) r -> p j r", j=PACK))
+
+        def load_words(a, tag):
+            tab_words[a] = tile("tab_words%d" % a, [P, T], I32, tag)
+            nc.sync.dma_start(tab_words[a][:], tab[a, 0:P * PACK * T].rearrange("(p c) -> p c", p=P).bitcast(I32))
+
+        load_down(0)
+        load_words(0, "words0")
+        load_down(1)
+
+        bias_rows = tile("bias_rows", [P, P], F32)
+        identity = tile("identity", [P, P], F32)
+        nc.gpsimd.memset(bias_rows[:], 0.0)
+        nc.gpsimd.dma_start(bias_rows[0:TILES, :], b.rearrange("(c p) -> c p", p=P))
+        make_identity(nc, identity[:])
+        w4_plane = tile("w4_plane", [P, PASSES, M], U8)
+        nc.gpsimd.memset(w4_plane[:].bitcast(I32), 0)
+        for quad in range(4):
+            nc.gpsimd.dma_start(
+                w4_plane[32 * quad:32 * quad + 4, :, :].bitcast(I32),
+                w4_scales[:, 4 * quad:4 * quad + 4, :].rearrange("a r n -> r a n").bitcast(I32))
+        warm = tile("warm", [P, 1], F32)
+        nc.scalar.activation(warm[:], identity[:, 0:1], SILU)
+        bias_ps = bps.tile([P, P], F32, name="bias_ps")
+        nc.tensor.transpose(bias_ps[:], bias_rows[:], identity[:])
+        bias = tile("bias", [P, TILES], F32)
+        nc.scalar.copy(bias[:], bias_ps[:, 0:TILES])
+
+        moved = tile("moved", [P, PASSES * S], U8)
+        nc.vector.memset(moved[:].bitcast(I32), 0)
+        pages = [tile("page%d" % i, [P, T], F32) for i in range(PAGES - 1)]
+        nc.vector.memset(pages[0][:], 0.0)
+        nc.vector.memset(pages[1][:], 0.0)
+
+        picked_scales = tile("picked_scales", [P, S], U8)
+        nc.vector.tensor_copy(picked_scales[:], tab_scales[:].indirect(pick[:]))
+
+        down_codes = [[None, None] for a in range(PASSES)]
+        down_planes = [[None, None] for a in range(PASSES)]
+
+        def cast_down(a, half, engine_copy):
+            grouped = tile("down_bf%d%d" % (a, half), [P, 2 * P * PACK], BF16)
+            engine_copy(
+                grouped[:].rearrange("p (t m j) -> p m j t", t=2, j=PACK),
+                down_raw[a][:].rearrange("p j (m t) -> p m j t", t=PACK)[:, :, :, 2 * half:2 * half + 2])
+            return grouped
+
+        def quantize(name, grouped, width):
+            codes = tile(name + "_codes", [P, width], U32)
+            plane = tile(name + "_plane", [P, width], U8)
+            nc.vector.quantize_mx(out=codes[:].bitcast(FP8X4), scales=plane[:], in_=grouped[:])
+            return codes, plane
+
+        def quantize_down(a, half, grouped):
+            down_codes[a][half], down_planes[a][half] = quantize("down%d%d" % (a, half), grouped, 2 * P)
+
+        picked = [tile("picked%d" % a, [P, S], U32) for a in range(PASSES)]
+
+        def gather_words(a, c0, width):
+            nc.vector.tensor_copy(
+                picked[a][:, c0:c0 + width],
+                tab_words[a][:].bitcast(U32).indirect(pick[:, c0 // LIST:(c0 + width) // LIST]))
+
+        def move_scales(a, quad):
+            nc.sync.dma_start(
+                moved[32 * quad:32 * quad + 4, a * S:(a + 1) * S].bitcast(I32),
+                picked_scales[16 * a + 4 * quad:16 * a + 4 * quad + 4, :].bitcast(I32))
+
+        moves = [(a, quad) for a in range(PASSES) for quad in range(4)]
+        for move in moves[:6]:
+            move_scales(*move)
+        load_words(1, "window")
+        for move in moves[6:]:
+            move_scales(*move)
+        g00 = cast_down(0, 0, nc.scalar.copy)
+        g01 = cast_down(0, 1, nc.scalar.copy)
+        planes = [moved[:, a * S:(a + 1) * S] for a in range(PASSES)]
+
+        up_rows = up.rearrange("(p j) n -> p j n", j=PACK)
+        w4_rows = w4_words.rearrange("a p c -> p a c")
+        late = tile("late_loads", [P, S + PACK * M], F32, "down_raw0")
+        gain = late[:, 0:S]
+        up_raw = {}
+
+        def load_up(first, count):
+            run = late[:, S + first * P * PACK:S + (first + count) * P * PACK]
+            up_raw[first] = run.rearrange("p (j n) -> p j n", j=PACK)
+            nc.sync.dma_start(up_raw[first], up_rows[:, :, first * P:(first + count) * P])
+
+        gather_words(0, 0, S)
+        quantize_down(0, 0, g00)
+        quantize_down(0, 1, g01)
+        load_up(*UP_GROUPS[0])
+        w4_head = tile("w4_head", [P, PASSES, 2 * 2 * P], U8, "down_bf00")
+        nc.sync.dma_start(w4_head[:].bitcast(I32), w4_rows[:, :, 0:512].bitcast(I32))
+        nc.sync.dma_start(gain[:, 0:256], wgo[:, 0:256])
+        load_up(*UP_GROUPS[1])
+        nc.sync.dma_start(gain[:, 256:S], wgo[:, 256:S])
+        load_up(*UP_GROUPS[2])
+        w4_rest = tile("w4_rest", [P, PASSES, (TILES - 2) * 2 * P], U8, "words0")
+        nc.sync.dma_start(w4_rest[:].bitcast(I32), w4_rows[:, :, 512:].bitcast(I32))
+        for group in UP_GROUPS[3:]:
+            load_up(*group)
+        g10 = cast_down(1, 0, nc.vector.tensor_copy)
+        g11 = cast_down(1, 1, nc.scalar.copy)
+        quantize_down(1, 0, g10)
+        quantize_down(1, 1, g11)
+
+        up_codes = {}
+
+        def prepare_up(first, count):
+            grouped = tile("up_bf%d" % first, [P, count * P * PACK], BF16, "late" if first + count == TILES else "")
+            nc.scalar.copy(
+                grouped[:].rearrange("p (c i j) -> p c j i", i=4, j=PACK),
+                up_raw[first].rearrange("p j (c i) -> p c j i", i=4))
+            codes, plane = quantize("up%d" % first, grouped, count * P)
+            for i in range(count):
+                up_codes[first + i] = (codes[:, i * P:(i + 1) * P], plane[:, i * P:(i + 1) * P])
+
+        for c0, width in LAST_GATHERS:
+            gather_words(1, c0, width)
+        prepare_up(*UP_GROUPS[0])
+
+        h_codes = {}
+
+        def make_h(c0, width):
+            grouped = tile("h_bf%d" % c0, [P, width * PACK], BF16)
+            for u0 in range(0, width, P):
+                cols = slice(c0 + u0, c0 + u0 + P)
+                acc = hps.tile([P, PACK, P], F32, name="h_acc")
+                for a in range(PASSES):
+                    for t in range(PACK):
+                        w = slice((t % 2) * P, (t % 2 + 1) * P)
+                        nc.tensor.matmul_mx(
+                            acc[:, t, :],
+                            lhsT=down_codes[a][t // 2][:, w].bitcast(FP8X4), lhsT_scale=down_planes[a][t // 2][:, w],
+                            rhs=picked[a][:, cols].bitcast(FP8X4), rhs_scale=planes[a][:, cols],
+                            start=(a == 0 and t == 0), stop=(a == PASSES - 1 and t == PACK - 1))
+                nc.scalar.copy(
+                    grouped[:, u0 * PACK:(u0 + P) * PACK].rearrange("p (c t) -> p c t", t=PACK),
+                    acc[:].rearrange("p t c -> p c t"))
+            h_codes[c0] = quantize("h%d" % c0, grouped, width)
+
+        values = [tile("values%d" % n, [P, S], F32) for n in range(TILES)]
+
+        def make_y(n, c0, width):
+            w4_tile, i = (w4_head, n) if n < 2 else (w4_rest, n - 2)
+            acc = yps.tile([P, BANK], F32, name="y_acc")
+            step = BANK if width == BANK else P
+            for u0 in range(0, width, step):
+                cols = slice(c0 + u0, c0 + u0 + step)
+                for a in range(PASSES):
+                    nc.tensor.matmul_mx(
+                        acc[:, u0:u0 + step],
+                        lhsT=w4_tile[:, a, 2 * P * i:2 * P * (i + 1)].bitcast(FP4X4),
+                        lhsT_scale=w4_plane[:, a, n * P:(n + 1) * P],
+                        rhs=picked[a][:, cols].bitcast(FP8X4), rhs_scale=planes[a][:, cols],
+                        start=(a == 0 and u0 == 0), stop=False)
+            pieces = [(s, w) for s, w in HEAD_CHUNKS if c0 <= s < c0 + width]
+            for s, w in pieces:
+                codes, plane = h_codes[s]
+                nc.tensor.matmul_mx(
+                    acc[:, s - c0:s - c0 + w],
+                    lhsT=up_codes[n][0].bitcast(FP8X4), lhsT_scale=up_codes[n][1],
+                    rhs=codes[:].bitcast(FP8X4), rhs_scale=plane[:],
+                    start=False, stop=(s == pieces[-1][0]))
+            nc.scalar.activation(values[n][:, c0:c0 + width], acc[:, 0:width], SILU, bias=bias[:, n:n + 1])
+
+        def scatter(n, c0, width):
+            nc.vector.tensor_tensor(
+                pages[n % PAGES][:].indirect(place[:, c0 // LIST:(c0 + width) // LIST]),
+                values[n][:, c0:c0 + width], gain[:, c0:c0 + width], MULT)
+
+        def store(n):
+            nc.sync.dma_start(out[n * P:(n + 1) * P, :], pages[n % PAGES][:])
+
+        for step, (c0, width) in enumerate(HEAD_CHUNKS):
+            make_h(c0, width)
+            make_y(0, c0, width)
+            scatter(0, c0, width)
+            if step == 0:
+                prepare_up(*UP_GROUPS[1])
+            make_y(1, c0, width)
+            scatter(1, c0, width)
+            if step >= 1:
+                prepare_up(*UP_GROUPS[step + 1])
+        pages.append(tile("page2", [P, T], F32, "late"))
+        nc.gpsimd.memset(pages[2][:], 0.0)
+        store(0)
+        store(1)
+        for n in range(2, TILES):
+            for c0 in range(0, S, BANK):
+                make_y(n, c0, BANK)
+            scatter(n, 0, S)
+            store(n)

@@ -27,6 +27,11 @@ HEAD_CHUNKS = ((0, 128), (128, 128), (256, 256), (512, 512))
 LAST_GATHERS = ((0, 256), (256, 256), (512, 512))
 UP_GROUPS = ((0, 1), (1, 1), (2, 2), (4, 2), (6, 2))
 PAGES = 3
+UP_AFTER = {2: "bias_first", 4: "h_bf512", 6: "bias_first"}
+H_AFTER = {128: "up_bf0", 256: "bias_first"}
+H_BANKS = ("bank_c", "bank_d", "bank_a", "bank_b", "bank_c", "bank_d", "bank_c", "bank_a")
+Y_BANKS = {(0, 0): "bank_c", (1, 0): "bank_d", (0, 128): "bank_a", (1, 128): "bank_b", (1, 256): "bank_a",
+           (0, 512): "bank_b", (1, 512): "bank_d"}
 
 
 def tile_list_tabhs_l_silu_kernel(
@@ -35,7 +40,6 @@ def tile_list_tabhs_l_silu_kernel(
     nc = tc.nc
     with ExitStack() as ctx:
         keep = ctx.enter_context(tc.tile_pool(name="keep", bufs=1))
-        hps = ctx.enter_context(tc.psum_pool(name="hps", bufs=3))
         yps = ctx.enter_context(tc.psum_pool(name="yps", bufs=4))
         bps = ctx.enter_context(tc.psum_pool(name="bps", bufs=1))
 
@@ -51,9 +55,8 @@ def tile_list_tabhs_l_silu_kernel(
             nc.sync.dma_start(
                 tab_scales[16 * a:16 * (a + 1), :].bitcast(I32),
                 tab[a, P * PACK * T:].rearrange("(q c) -> q c", q=16).bitcast(I32))
-        nc.sync.dma_start(place[:], offs2)
-        nc.gpsimd.memset(tab_scales[32:64, :].bitcast(I32), 0)
-        nc.gpsimd.memset(tab_scales[64:128, :].bitcast(I32), 0)
+        nc.vector.memset(tab_scales[32:64, :].bitcast(I32), 0)
+        nc.vector.memset(tab_scales[64:128, :].bitcast(I32), 0)
 
         down_raw = [tile("down_raw%d" % a, [P, PACK, R], F32) for a in range(PASSES)]
         tab_words = {}
@@ -65,33 +68,31 @@ def tile_list_tabhs_l_silu_kernel(
             tab_words[a] = tile("tab_words%d" % a, [P, T], I32, tag)
             nc.sync.dma_start(tab_words[a][:], tab[a, 0:P * PACK * T].rearrange("(p c) -> p c", p=P).bitcast(I32))
 
-        load_down(0)
         load_words(0, "words0")
+        load_down(0)
         load_down(1)
+        nc.sync.dma_start(place[:], offs2)
 
         bias_rows = tile("bias_rows", [P, P], F32)
         identity = tile("identity", [P, P], F32)
         nc.gpsimd.memset(bias_rows[:], 0.0)
         nc.gpsimd.dma_start(bias_rows[0:TILES, :], b.rearrange("(c p) -> c p", p=P))
         make_identity(nc, identity[:])
-        w4_plane = tile("w4_plane", [P, PASSES, M], U8)
-        nc.gpsimd.memset(w4_plane[:].bitcast(I32), 0)
-        for quad in range(4):
-            nc.gpsimd.dma_start(
-                w4_plane[32 * quad:32 * quad + 4, :, :].bitcast(I32),
-                w4_scales[:, 4 * quad:4 * quad + 4, :].rearrange("a r n -> r a n").bitcast(I32))
-        warm = tile("warm", [P, 1], F32)
-        nc.scalar.activation(warm[:], identity[:, 0:1], SILU)
-        bias_ps = bps.tile([P, P], F32, name="bias_ps")
-        nc.tensor.transpose(bias_ps[:], bias_rows[:], identity[:])
-        bias = tile("bias", [P, TILES], F32)
-        nc.scalar.copy(bias[:], bias_ps[:, 0:TILES])
 
         moved = tile("moved", [P, PASSES * S], U8)
         nc.vector.memset(moved[:].bitcast(I32), 0)
-        pages = [tile("page%d" % i, [P, T], F32) for i in range(PAGES - 1)]
+        pages = [tile("page%d" % i, [P, T], F32) for i in range(PAGES)]
         nc.vector.memset(pages[0][:], 0.0)
+        warm = tile("warm", [P, 1], F32)
+        nc.scalar.activation(warm[:], pages[0][:, 0:1], SILU)
         nc.vector.memset(pages[1][:], 0.0)
+
+        bias_ps = bps.tile([P, P], F32, name="bias_ps", tag="bank_a")
+        nc.tensor.transpose(bias_ps[:], bias_rows[:], identity[:])
+        bias = tile("bias", [P, TILES], F32)
+        nc.scalar.copy(bias[:], bias_ps[:, 0:TILES])
+        bias_first = tile("bias_first", [P, 2], F32)
+        nc.scalar.copy(bias_first[:], bias_ps[:, 0:2])
 
         picked_scales = tile("picked_scales", [P, S], U8)
         nc.vector.tensor_copy(picked_scales[:], tab_scales[:].indirect(pick[:]))
@@ -102,8 +103,8 @@ def tile_list_tabhs_l_silu_kernel(
         def cast_down(a, half, engine_copy):
             grouped = tile("down_bf%d%d" % (a, half), [P, 2 * P * PACK], BF16)
             engine_copy(
-                grouped[:].rearrange("p (t m j) -> p m j t", t=2, j=PACK),
-                down_raw[a][:].rearrange("p j (m t) -> p m j t", t=PACK)[:, :, :, 2 * half:2 * half + 2])
+                grouped[:].rearrange("p (t m j) -> p m t j", t=2, j=PACK),
+                down_raw[a][:].rearrange("p j (m t) -> p m t j", t=PACK)[:, :, 2 * half:2 * half + 2, :])
             return grouped
 
         def quantize(name, grouped, width):
@@ -128,10 +129,10 @@ def tile_list_tabhs_l_silu_kernel(
                 picked_scales[16 * a + 4 * quad:16 * a + 4 * quad + 4, :].bitcast(I32))
 
         moves = [(a, quad) for a in range(PASSES) for quad in range(4)]
-        for move in moves[:6]:
+        for move in moves[:5]:
             move_scales(*move)
         load_words(1, "window")
-        for move in moves[6:]:
+        for move in moves[5:]:
             move_scales(*move)
         g00 = cast_down(0, 0, nc.scalar.copy)
         g01 = cast_down(0, 1, nc.scalar.copy)
@@ -139,56 +140,66 @@ def tile_list_tabhs_l_silu_kernel(
 
         up_rows = up.rearrange("(p j) n -> p j n", j=PACK)
         w4_rows = w4_words.rearrange("a p c -> p a c")
-        late = tile("late_loads", [P, S + PACK * M], F32, "down_raw0")
-        gain = late[:, 0:S]
         up_raw = {}
 
         def load_up(first, count):
-            run = late[:, S + first * P * PACK:S + (first + count) * P * PACK]
+            if first == 0:
+                run = tile("up_first", [P, count * P * PACK], F32, "words0")[:]
+            else:
+                run = late[:, S + (first - 1) * P * PACK:S + (first - 1 + count) * P * PACK]
             up_raw[first] = run.rearrange("p (j n) -> p j n", j=PACK)
             nc.sync.dma_start(up_raw[first], up_rows[:, :, first * P:(first + count) * P])
 
         gather_words(0, 0, S)
+        nc.vector.memset(pages[2][:], 0.0)
         quantize_down(0, 0, g00)
+        w4_plane = tile("w4_plane", [P, PASSES, M], U8, "down_bf00")
+        nc.vector.memset(w4_plane[:].bitcast(I32), 0)
         quantize_down(0, 1, g01)
         load_up(*UP_GROUPS[0])
-        w4_head = tile("w4_head", [P, PASSES, 2 * 2 * P], U8, "down_bf00")
+        for quad in range(4):
+            nc.sync.dma_start(
+                w4_plane[32 * quad:32 * quad + 4, :, :].bitcast(I32),
+                w4_scales[:, 4 * quad:4 * quad + 4, :].rearrange("a r n -> r a n").bitcast(I32))
+        w4_head = tile("w4_head", [P, PASSES, 2 * 2 * P], U8, "down_raw0")
         nc.sync.dma_start(w4_head[:].bitcast(I32), w4_rows[:, :, 0:512].bitcast(I32))
+        g10 = cast_down(1, 0, nc.vector.tensor_copy)
+        g11 = cast_down(1, 1, nc.scalar.copy)
+        late = tile("late_loads", [P, S + PACK * (M - P)], F32, "down_raw1")
+        gain = late[:, 0:S]
         nc.sync.dma_start(gain[:, 0:256], wgo[:, 0:256])
         load_up(*UP_GROUPS[1])
         nc.sync.dma_start(gain[:, 256:S], wgo[:, 256:S])
         load_up(*UP_GROUPS[2])
-        w4_rest = tile("w4_rest", [P, PASSES, (TILES - 2) * 2 * P], U8, "words0")
-        nc.sync.dma_start(w4_rest[:].bitcast(I32), w4_rows[:, :, 512:].bitcast(I32))
         for group in UP_GROUPS[3:]:
             load_up(*group)
-        g10 = cast_down(1, 0, nc.vector.tensor_copy)
-        g11 = cast_down(1, 1, nc.scalar.copy)
         quantize_down(1, 0, g10)
         quantize_down(1, 1, g11)
 
         up_codes = {}
 
         def prepare_up(first, count):
-            grouped = tile("up_bf%d" % first, [P, count * P * PACK], BF16, "late" if first + count == TILES else "")
-            nc.scalar.copy(
-                grouped[:].rearrange("p (c i j) -> p c j i", i=4, j=PACK),
-                up_raw[first].rearrange("p j (c i) -> p c j i", i=4))
+            grouped = tile("up_bf%d" % first, [P, count * P * PACK], BF16, UP_AFTER.get(first, ""))
+            for i in range(count):
+                nc.scalar.copy(
+                    grouped[:, i * P * PACK:(i + 1) * P * PACK].rearrange("p (c i j) -> p c j i", i=4, j=PACK),
+                    up_raw[first][:, :, i * P:(i + 1) * P].rearrange("p j (c i) -> p c j i", i=4))
             codes, plane = quantize("up%d" % first, grouped, count * P)
             for i in range(count):
                 up_codes[first + i] = (codes[:, i * P:(i + 1) * P], plane[:, i * P:(i + 1) * P])
 
         for c0, width in LAST_GATHERS:
             gather_words(1, c0, width)
-        prepare_up(*UP_GROUPS[0])
+        w4_rest = tile("w4_rest", [P, PASSES, (TILES - 2) * 2 * P], U8, "window")
+        nc.sync.dma_start(w4_rest[:].bitcast(I32), w4_rows[:, :, 512:].bitcast(I32))
 
         h_codes = {}
 
         def make_h(c0, width):
-            grouped = tile("h_bf%d" % c0, [P, width * PACK], BF16)
+            grouped = tile("h_bf%d" % c0, [P, width * PACK], BF16, H_AFTER.get(c0, ""))
             for u0 in range(0, width, P):
                 cols = slice(c0 + u0, c0 + u0 + P)
-                acc = hps.tile([P, PACK, P], F32, name="h_acc")
+                acc = bps.tile([P, PACK, P], F32, name="h_acc", tag=H_BANKS[(c0 + u0) // P])
                 for a in range(PASSES):
                     for t in range(PACK):
                         w = slice((t % 2) * P, (t % 2 + 1) * P)
@@ -206,26 +217,28 @@ def tile_list_tabhs_l_silu_kernel(
 
         def make_y(n, c0, width):
             w4_tile, i = (w4_head, n) if n < 2 else (w4_rest, n - 2)
-            acc = yps.tile([P, BANK], F32, name="y_acc")
+            tag = Y_BANKS.get((n, c0))
+            if tag:
+                acc = bps.tile([P, BANK], F32, name="y_held", tag=tag)
+            else:
+                acc = yps.tile([P, BANK], F32, name="y_acc")
             step = BANK if width == BANK else P
+            base, adapter = [], []
             for u0 in range(0, width, step):
                 cols = slice(c0 + u0, c0 + u0 + step)
-                for a in range(PASSES):
-                    nc.tensor.matmul_mx(
-                        acc[:, u0:u0 + step],
-                        lhsT=w4_tile[:, a, 2 * P * i:2 * P * (i + 1)].bitcast(FP4X4),
-                        lhsT_scale=w4_plane[:, a, n * P:(n + 1) * P],
-                        rhs=picked[a][:, cols].bitcast(FP8X4), rhs_scale=planes[a][:, cols],
-                        start=(a == 0 and u0 == 0), stop=False)
-            pieces = [(s, w) for s, w in HEAD_CHUNKS if c0 <= s < c0 + width]
-            for s, w in pieces:
-                codes, plane = h_codes[s]
-                nc.tensor.matmul_mx(
-                    acc[:, s - c0:s - c0 + w],
-                    lhsT=up_codes[n][0].bitcast(FP8X4), lhsT_scale=up_codes[n][1],
-                    rhs=codes[:].bitcast(FP8X4), rhs_scale=plane[:],
-                    start=False, stop=(s == pieces[-1][0]))
-            nc.scalar.activation(values[n][:, c0:c0 + width], acc[:, 0:width], SILU, bias=bias[:, n:n + 1])
+                for a in reversed(range(PASSES)):
+                    base.append((acc[:, u0:u0 + step], w4_tile[:, a, 2 * P * i:2 * P * (i + 1)].bitcast(FP4X4),
+                                 w4_plane[:, a, n * P:(n + 1) * P], picked[a][:, cols].bitcast(FP8X4), planes[a][:, cols]))
+            for s, w in HEAD_CHUNKS:
+                if c0 <= s < c0 + width:
+                    adapter.append((acc[:, s - c0:s - c0 + w], up_codes[n][0].bitcast(FP8X4), up_codes[n][1],
+                                    h_codes[s][0][:].bitcast(FP8X4), h_codes[s][1][:]))
+            passes = base + adapter if tag else adapter + base
+            for k, (dst, lhs, lhs_plane, rhs, rhs_plane) in enumerate(passes):
+                nc.tensor.matmul_mx(dst, lhsT=lhs, lhsT_scale=lhs_plane, rhs=rhs, rhs_scale=rhs_plane,
+                                    start=(k == 0), stop=(k == len(passes) - 1))
+            nc.scalar.activation(values[n][:, c0:c0 + width], acc[:, 0:width], SILU,
+                                 bias=(bias_first if n < 2 and c0 == 0 else bias)[:, n:n + 1])
 
         def scatter(n, c0, width):
             nc.vector.tensor_tensor(
@@ -235,22 +248,25 @@ def tile_list_tabhs_l_silu_kernel(
         def store(n):
             nc.sync.dma_start(out[n * P:(n + 1) * P, :], pages[n % PAGES][:])
 
+        make_h(*HEAD_CHUNKS[0])
+        prepare_up(*UP_GROUPS[0])
         for step, (c0, width) in enumerate(HEAD_CHUNKS):
-            make_h(c0, width)
+            if step + 1 < len(HEAD_CHUNKS):
+                make_h(*HEAD_CHUNKS[step + 1])
             make_y(0, c0, width)
             scatter(0, c0, width)
             if step == 0:
                 prepare_up(*UP_GROUPS[1])
             make_y(1, c0, width)
             scatter(1, c0, width)
-            if step >= 1:
-                prepare_up(*UP_GROUPS[step + 1])
-        pages.append(tile("page2", [P, T], F32, "late"))
-        nc.gpsimd.memset(pages[2][:], 0.0)
+            if step >= 2:
+                prepare_up(*UP_GROUPS[step])
         store(0)
         store(1)
         for n in range(2, TILES):
             for c0 in range(0, S, BANK):
                 make_y(n, c0, BANK)
+            if n == 2:
+                prepare_up(*UP_GROUPS[4])
             scatter(n, 0, S)
             store(n)

from contextlib import ExitStack

import concourse.mybir as mybir
from concourse.masks import make_identity

K, M, T, S, R = 1024, 1024, 2048, 1024, 512
FLOPS = 2 * K * M * S + 2 * K * R * S + 2 * R * M * S

F32 = mybir.dt.float32
BF16 = mybir.dt.bfloat16
I32 = mybir.dt.int32
U32 = mybir.dt.uint32
U16 = mybir.dt.uint16
U8 = mybir.dt.uint8
FP8X4 = mybir.dt.float8_e4m3fn_x4
FP4X4 = mybir.dt.float4_e2m1fn_x4
SILU = mybir.ActivationFunctionType.Silu
MULT = mybir.AluOpType.mult

P = 128
PACK = 4
PASSES = K // (P * PACK)
TILES = M // P
LIST = 16
BANK = 512
HEAD_CHUNKS = ((0, 128), (128, 128), (256, 256), (512, 512))
LAST_GATHERS = ((0, 256), (256, 256), (512, 512))
UP_GROUPS = ((0, 1), (1, 1), (2, 2), (4, 2), (6, 2))
PAGES = 3
UP_AFTER = {2: "bias_first", 4: "h_bf512", 6: "bias_first"}
H_AFTER = {128: "up_bf0", 256: "bias_first"}
H_BANKS = ("bank_c", "bank_d", "bank_a", "bank_b", "bank_c", "bank_d", "bank_c", "bank_a")
Y_BANKS = {(0, 0): "bank_c", (1, 0): "bank_d", (0, 128): "bank_a", (1, 128): "bank_b", (1, 256): "bank_a",
           (0, 512): "bank_b", (1, 512): "bank_d"}


def tile_list_tabhs_l_silu_kernel(
    tc, tab, w4_words, w4_scales, down, up, b, wgo, offs, offs2, out
):
    nc = tc.nc
    with ExitStack() as ctx:
        keep = ctx.enter_context(tc.tile_pool(name="keep", bufs=1))
        yps = ctx.enter_context(tc.psum_pool(name="yps", bufs=4))
        bps = ctx.enter_context(tc.psum_pool(name="bps", bufs=1))

        def tile(name, shape, dtype, tag=""):
            return keep.tile(shape, dtype, name=name, tag=tag or name, align_bytes=64)

        pick = keep.tile([P, S // LIST], U16, name="pick")
        place = keep.tile([P, S // LIST], U16, name="place")
        nc.sync.dma_start(pick[:], offs)

        tab_scales = tile("tab_scales", [P, T], U8, "window")
        for a in range(PASSES):
            nc.sync.dma_start(
                tab_scales[16 * a:16 * (a + 1), :].bitcast(I32),
                tab[a, P * PACK * T:].rearrange("(q c) -> q c", q=16).bitcast(I32))
        nc.vector.memset(tab_scales[32:64, :].bitcast(I32), 0)
        nc.vector.memset(tab_scales[64:128, :].bitcast(I32), 0)

        down_raw = [tile("down_raw%d" % a, [P, PACK, R], F32) for a in range(PASSES)]
        tab_words = {}

        def load_down(a):
            nc.sync.dma_start(down_raw[a][:], down[512 * a:512 * (a + 1), :].rearrange("(p j) r -> p j r", j=PACK))

        def load_words(a, tag):
            tab_words[a] = tile("tab_words%d" % a, [P, T], I32, tag)
            nc.sync.dma_start(tab_words[a][:], tab[a, 0:P * PACK * T].rearrange("(p c) -> p c", p=P).bitcast(I32))

        load_words(0, "words0")
        load_down(0)
        load_down(1)
        nc.sync.dma_start(place[:], offs2)

        bias_rows = tile("bias_rows", [P, P], F32)
        identity = tile("identity", [P, P], F32)
        nc.gpsimd.memset(bias_rows[:], 0.0)
        nc.gpsimd.dma_start(bias_rows[0:TILES, :], b.rearrange("(c p) -> c p", p=P))
        make_identity(nc, identity[:])

        moved = tile("moved", [P, PASSES * S], U8)
        nc.vector.memset(moved[:].bitcast(I32), 0)
        pages = [tile("page%d" % i, [P, T], F32) for i in range(PAGES)]
        nc.vector.memset(pages[0][:], 0.0)
        warm = tile("warm", [P, 1], F32)
        nc.scalar.activation(warm[:], pages[0][:, 0:1], SILU)
        nc.vector.memset(pages[1][:], 0.0)

        bias_ps = bps.tile([P, P], F32, name="bias_ps", tag="bank_a")
        nc.tensor.transpose(bias_ps[:], bias_rows[:], identity[:])
        bias = tile("bias", [P, TILES], F32)
        nc.scalar.copy(bias[:], bias_ps[:, 0:TILES])
        bias_first = tile("bias_first", [P, 2], F32)
        nc.scalar.copy(bias_first[:], bias_ps[:, 0:2])

        picked_scales = tile("picked_scales", [P, S], U8)
        nc.vector.tensor_copy(picked_scales[:], tab_scales[:].indirect(pick[:]))

        down_codes = [[None, None] for a in range(PASSES)]
        down_planes = [[None, None] for a in range(PASSES)]

        def cast_down(a, half, engine_copy):
            grouped = tile("down_bf%d%d" % (a, half), [P, 2 * P * PACK], BF16)
            engine_copy(
                grouped[:].rearrange("p (t m j) -> p m t j", t=2, j=PACK),
                down_raw[a][:].rearrange("p j (m t) -> p m t j", t=PACK)[:, :, 2 * half:2 * half + 2, :])
            return grouped

        def quantize(name, grouped, width):
            codes = tile(name + "_codes", [P, width], U32)
            plane = tile(name + "_plane", [P, width], U8)
            nc.vector.quantize_mx(out=codes[:].bitcast(FP8X4), scales=plane[:], in_=grouped[:])
            return codes, plane

        def quantize_down(a, half, grouped):
            down_codes[a][half], down_planes[a][half] = quantize("down%d%d" % (a, half), grouped, 2 * P)

        picked = [tile("picked%d" % a, [P, S], U32) for a in range(PASSES)]

        def gather_words(a, c0, width):
            nc.vector.tensor_copy(
                picked[a][:, c0:c0 + width],
                tab_words[a][:].bitcast(U32).indirect(pick[:, c0 // LIST:(c0 + width) // LIST]))

        def move_scales(a, quad):
            nc.sync.dma_start(
                moved[32 * quad:32 * quad + 4, a * S:(a + 1) * S].bitcast(I32),
                picked_scales[16 * a + 4 * quad:16 * a + 4 * quad + 4, :].bitcast(I32))

        moves = [(a, quad) for a in range(PASSES) for quad in range(4)]
        for move in moves[:5]:
            move_scales(*move)
        load_words(1, "window")
        for move in moves[5:]:
            move_scales(*move)
        g00 = cast_down(0, 0, nc.scalar.copy)
        g01 = cast_down(0, 1, nc.scalar.copy)
        planes = [moved[:, a * S:(a + 1) * S] for a in range(PASSES)]

        up_rows = up.rearrange("(p j) n -> p j n", j=PACK)
        w4_rows = w4_words.rearrange("a p c -> p a c")
        up_raw = {}

        def load_up(first, count):
            if first == 0:
                run = tile("up_first", [P, count * P * PACK], F32, "words0")[:]
            else:
                run = late[:, S + (first - 1) * P * PACK:S + (first - 1 + count) * P * PACK]
            up_raw[first] = run.rearrange("p (j n) -> p j n", j=PACK)
            nc.sync.dma_start(up_raw[first], up_rows[:, :, first * P:(first + count) * P])

        gather_words(0, 0, S)
        nc.vector.memset(pages[2][:], 0.0)
        quantize_down(0, 0, g00)
        w4_plane = tile("w4_plane", [P, PASSES, M], U8, "down_bf00")
        nc.vector.memset(w4_plane[:].bitcast(I32), 0)
        quantize_down(0, 1, g01)
        load_up(*UP_GROUPS[0])
        for quad in range(4):
            nc.sync.dma_start(
                w4_plane[32 * quad:32 * quad + 4, :, :].bitcast(I32),
                w4_scales[:, 4 * quad:4 * quad + 4, :].rearrange("a r n -> r a n").bitcast(I32))
        w4_head = tile("w4_head", [P, PASSES, 2 * 2 * P], U8, "down_raw0")
        nc.sync.dma_start(w4_head[:].bitcast(I32), w4_rows[:, :, 0:512].bitcast(I32))
        g10 = cast_down(1, 0, nc.vector.tensor_copy)
        g11 = cast_down(1, 1, nc.scalar.copy)
        late = tile("late_loads", [P, S + PACK * (M - P)], F32, "down_raw1")
        gain = late[:, 0:S]
        nc.sync.dma_start(gain[:, 0:256], wgo[:, 0:256])
        load_up(*UP_GROUPS[1])
        nc.sync.dma_start(gain[:, 256:S], wgo[:, 256:S])
        load_up(*UP_GROUPS[2])
        for group in UP_GROUPS[3:]:
            load_up(*group)
        quantize_down(1, 0, g10)
        quantize_down(1, 1, g11)

        up_codes = {}

        def prepare_up(first, count):
            grouped = tile("up_bf%d" % first, [P, count * P * PACK], BF16, UP_AFTER.get(first, ""))
            for i in range(count):
                nc.scalar.copy(
                    grouped[:, i * P * PACK:(i + 1) * P * PACK].rearrange("p (c i j) -> p c j i", i=4, j=PACK),
                    up_raw[first][:, :, i * P:(i + 1) * P].rearrange("p j (c i) -> p c j i", i=4))
            codes, plane = quantize("up%d" % first, grouped, count * P)
            for i in range(count):
                up_codes[first + i] = (codes[:, i * P:(i + 1) * P], plane[:, i * P:(i + 1) * P])

        for c0, width in LAST_GATHERS:
            gather_words(1, c0, width)
        w4_rest = tile("w4_rest", [P, PASSES, (TILES - 2) * 2 * P], U8, "window")
        nc.sync.dma_start(w4_rest[:].bitcast(I32), w4_rows[:, :, 512:].bitcast(I32))

        h_codes = {}

        def make_h(c0, width):
            grouped = tile("h_bf%d" % c0, [P, width * PACK], BF16, H_AFTER.get(c0, ""))
            for u0 in range(0, width, P):
                cols = slice(c0 + u0, c0 + u0 + P)
                acc = bps.tile([P, PACK, P], F32, name="h_acc", tag=H_BANKS[(c0 + u0) // P])
                for a in range(PASSES):
                    for t in range(PACK):
                        w = slice((t % 2) * P, (t % 2 + 1) * P)
                        nc.tensor.matmul_mx(
                            acc[:, t, :],
                            lhsT=down_codes[a][t // 2][:, w].bitcast(FP8X4), lhsT_scale=down_planes[a][t // 2][:, w],
                            rhs=picked[a][:, cols].bitcast(FP8X4), rhs_scale=planes[a][:, cols],
                            start=(a == 0 and t == 0), stop=(a == PASSES - 1 and t == PACK - 1))
                nc.scalar.copy(
                    grouped[:, u0 * PACK:(u0 + P) * PACK].rearrange("p (c t) -> p c t", t=PACK),
                    acc[:].rearrange("p t c -> p c t"))
            h_codes[c0] = quantize("h%d" % c0, grouped, width)

        values = [tile("values%d" % n, [P, S], F32) for n in range(TILES)]

        def make_y(n, c0, width):
            w4_tile, i = (w4_head, n) if n < 2 else (w4_rest, n - 2)
            tag = Y_BANKS.get((n, c0))
            if tag:
                acc = bps.tile([P, BANK], F32, name="y_held", tag=tag)
            else:
                acc = yps.tile([P, BANK], F32, name="y_acc")
            step = BANK if width == BANK else P
            base, adapter = [], []
            for u0 in range(0, width, step):
                cols = slice(c0 + u0, c0 + u0 + step)
                for a in reversed(range(PASSES)):
                    base.append((acc[:, u0:u0 + step], w4_tile[:, a, 2 * P * i:2 * P * (i + 1)].bitcast(FP4X4),
                                 w4_plane[:, a, n * P:(n + 1) * P], picked[a][:, cols].bitcast(FP8X4), planes[a][:, cols]))
            for s, w in HEAD_CHUNKS:
                if c0 <= s < c0 + width:
                    adapter.append((acc[:, s - c0:s - c0 + w], up_codes[n][0].bitcast(FP8X4), up_codes[n][1],
                                    h_codes[s][0][:].bitcast(FP8X4), h_codes[s][1][:]))
            passes = base + adapter if tag else adapter + base
            for k, (dst, lhs, lhs_plane, rhs, rhs_plane) in enumerate(passes):
                nc.tensor.matmul_mx(dst, lhsT=lhs, lhsT_scale=lhs_plane, rhs=rhs, rhs_scale=rhs_plane,
                                    start=(k == 0), stop=(k == len(passes) - 1))
            nc.scalar.activation(values[n][:, c0:c0 + width], acc[:, 0:width], SILU,
                                 bias=(bias_first if n < 2 and c0 == 0 else bias)[:, n:n + 1])

        def scatter(n, c0, width):
            nc.vector.tensor_tensor(
                pages[n % PAGES][:].indirect(place[:, c0 // LIST:(c0 + width) // LIST]),
                values[n][:, c0:c0 + width], gain[:, c0:c0 + width], MULT)

        def store(n):
            nc.sync.dma_start(out[n * P:(n + 1) * P, :], pages[n % PAGES][:])

        make_h(*HEAD_CHUNKS[0])
        prepare_up(*UP_GROUPS[0])
        for step, (c0, width) in enumerate(HEAD_CHUNKS):
            if step + 1 < len(HEAD_CHUNKS):
                make_h(*HEAD_CHUNKS[step + 1])
            make_y(0, c0, width)
            scatter(0, c0, width)
            if step == 0:
                prepare_up(*UP_GROUPS[1])
            make_y(1, c0, width)
            scatter(1, c0, width)
            if step >= 2:
                prepare_up(*UP_GROUPS[step])
        store(0)
        store(1)
        for n in range(2, TILES):
            for c0 in range(0, S, BANK):
                make_y(n, c0, BANK)
            if n == 2:
                prepare_up(*UP_GROUPS[4])
            scatter(n, 0, S)
            store(n)
